import numpy as np, ml_dtypes
CORES = [66,74,82,90,194,202,210,218]
N = 8
BF = ml_dtypes.bfloat16
def gentries(a):
    return np.ascontiguousarray(a.reshape(8, 16, -1).transpose(0, 2, 1)).reshape(8, -1)
def gtable(e):
    e = np.asarray(e); return np.ascontiguousarray(e.reshape(8, -1, 16).transpose(0, 2, 1)).reshape(128, -1).astype(np.int32)
V, K, RO = 1024, 4, 3
W = N * V
def apart(rng, M, n=8):
    s = []
    for j in range(M - K, M):
        t = rng.integers(0, j + 1, (n, W)); clash = np.zeros((n, W), bool)
        for a in s: clash |= a == t
        s.append(np.where(clash, j, t))
    return np.stack(s, 1)
def far(rng):
    return (np.arange(W) + 1 + apart(rng, W - 1)) % W
def near(rng, h):
    t = apart(rng, 2 * h); return (np.arange(W) + np.where(t < h, t - h, t - h + 1)) % W
def mixed(rng):
    share = np.repeat(rng.choice(np.array([0.05, 0.2, 0.5]), (8, 1, N)), V, axis=2)
    return np.where(rng.random((8, 1, W)) < share, near(rng, 8), far(rng))
def points(rng):
    cen = rng.integers(0, 256, (8, 16, 48)); lab = rng.integers(0, 48, (8, W))
    noise = rng.standard_normal((8, 16, W)) * np.exp2(rng.integers(1, 6, (8, 1, W)))
    return np.clip(np.rint(np.take_along_axis(cen, lab[:, None, :], 2) + noise), 0, 255).astype(np.int64)
def stairs(rng, X, nb):
    z = rng.integers(0, 256) + 256 * rng.permutation(W // 256); o = np.concatenate([z, rng.permutation(np.setdiff1d(np.arange(W), z))])
    Q = o[:K * (K + 1)].reshape(K + 1, K)[::-1].T; P = o[K * (K + 1):K * (K + 1) + W // 16]; j = np.arange(K)
    X[:, P] = 0; nb[:, P] = Q[:, :1]
    for s in range(K):
        for t in range(K + 1):
            X[:, Q[s, t]] = (4080 - K * t - s + np.arange(16)) // 16
            nb[(s + t + j) % K, Q[s, t]] = Q[s, (t + 1 + j) % (K + 1)]
def pack(X, nb):
    x = np.ascontiguousarray(X.reshape(8, 16, N, V).transpose(2, 0, 1, 3)).reshape(N, 128, V)
    e = np.ascontiguousarray(nb.reshape(8, K, N, V).transpose(2, 0, 1, 3)).reshape(N, 8, K * V)
    return {"x": x.astype(np.float32).astype(BF), "nb": np.stack([gtable(a) for a in e])}
def setup_inputs(rng):
    return pack(points(rng), mixed(rng))
def setup_inputs_ties(rng):
    q = rng.permutation(8); X = rng.integers(0, 2, (8, 16, W)); nb = mixed(rng)
    X[q[0]] = 255 * rng.integers(0, 2, (1, W)); X[q[1]] = rng.integers(0, 256, (16, 1)); X[q[2]] = rng.integers(0, 4, (16, W))
    X[q[3]] = 255 * rng.integers(0, 2, (16, W)); X[q[4]] = 100 * (np.arange(16)[:, None] == rng.integers(0, 16, (1, W)))
    stairs(rng, X[int(q[5])], nb[int(q[5])])
    return pack(X, nb)
def setup_inputs_ring(rng):
    nb = np.zeros((8, K, W), np.int64); h = np.array([0, 1, 0, 2])[:K, None]; m = np.array([1, 1, 2, 2])[:K, None]
    for g in range(8):
        p = rng.permutation(W); pos = np.argsort(p)
        e = ((((pos - h) % W) ^ m) + h) % W
        nb[g] = p[e][rng.permutation(K)]
    return pack(points(rng), nb)
def setup_inputs_hubs(rng):
    X = points(rng); nb = np.zeros((8, K, W), np.int64); H = 2 * K + 1; ends = np.array([0, V - 1, V, W - 1]); q = rng.permutation(8); remote = q[:2]
    for g in range(8):
        o = rng.permutation(np.setdiff1d(np.arange(W), ends)); hub = rng.permutation(np.concatenate([ends, o[:H - 4]])); P = o[H - 4:H - 4 + W // 16]
        m = rng.integers(0, H, W); m[hub] = np.arange(H); k = (m + 1 + apart(rng, H - 1, 1)[0]) % H
        if g in remote:
            X[g] = rng.integers(200, 256, (16, W)); X[g][:, hub] = rng.integers(0, 32, (16, H))
        k[:, hub[0]] = np.array([4, 1, 2, 3])[:K]; k[:, hub[1]] = np.array([0, 4, 2, 3])[:K]; k[:, P] = np.arange(K)[:, None]
        nb[g] = hub[k]; X[g][0, hub[:4]] = 255; X[g][0, hub[4]] = 0; X[g][:, P] = X[g][:, hub[4:5]]
    g = int(q[2]); h = int(rng.integers(0, W)); a = int(rng.integers(0, K)); others = np.arange(W) != h
    e = far(rng)[g]; e = np.where(others & (e == h), e[a], e); e[a, others] = h
    nb[g] = e; X[g][:, h] = 255; X[g][:, int(e[a, h])] = 128
    return pack(X, nb)
def setup_inputs_away(rng):
    sh = (np.arange(8) + rng.integers(0, N)) % N; q = rng.permutation(N); g = int(rng.choice(np.flatnonzero(sh))); u = np.arange(W); X = points(rng)
    to = (np.arange(N)[None, :] + sh[:, None]) % N
    to[:, q[1:1 + N // 2]] = q[0]; to[g] = q[0]; to[g, q[0]] = q[1]
    base = to[:, u // V][:, None, :] * V
    nb = base + (u % V + 1 + apart(rng, V - 1)) % V
    o = rng.permutation(V); at = np.argsort(o)
    nb[g] = base[g] + o[(at[u % V] + 1 + np.arange(K)[:, None]) % V]
    X[g] = np.where(u // V == q[0], 192, 0) + rng.integers(0, 64, (16, W))
    return pack(X, nb)
def setup_inputs_spread(rng):
    X = (np.exp2(8 * rng.random((8, 1, W))) * rng.random((8, 16, W)) * (rng.random((8, 1, W)) > 0.0625)).astype(np.int64)
    nb = far(rng); u = np.arange(W)
    for g in rng.permutation(8)[:2]:
        for i in range(K):
            o = rng.permutation(V); at = np.argsort(o)
            nb[g, i] = (u // V + 1 + i) % N * V + o[(at[u % V] + 1) % V]
    return pack(X, nb)
def check_inputs(d):
    bad = []; x = np.asarray(d["x"]).astype(np.float32)
    if not np.all((x >= 0) & (x <= 255) & (x == np.floor(x))): bad.append("whole numbers of x")
    e = np.stack([gentries(a) for a in d["nb"]]).astype(np.int64).reshape(N, 8, K, V)
    if np.min(e) < 0 or np.max(e) > W - 1: bad.append("range of nb")
    s = np.sort(e, axis=2)
    if np.any(s[:, :, 1:] == s[:, :, :-1]): bad.append("different neighbours")
    if np.any(e == np.arange(W).reshape(N, 1, 1, V)): bad.append("no point its own neighbour")
    return bad
def reference(x, nb):
    X = np.ascontiguousarray(x.astype(np.float32).astype(np.int64).reshape(N, 8, 16, V).transpose(1, 2, 0, 3)).reshape(8, 16, W)
    b = np.stack([gentries(a) for a in nb]).astype(np.int64).reshape(N, 8, K, V)
    b = np.ascontiguousarray(b.transpose(1, 2, 0, 3)).reshape(8, K, W)
    def dist(c):
        return np.add.reduce(np.abs(X - np.take_along_axis(X, c[:, None, :], 2)), axis=1)
    d = np.stack([dist(b[:, i]) for i in range(K)], 1); u = np.arange(W)[None, :]; slot = np.arange(K)[None, :, None]
    for t in range(RO):
        old = b.copy()
        for i in range(K):
            c = np.take_along_axis(old[:, (i + t) & (K - 1)], old[:, i], 1); e = dist(c)
            s = np.argmax(d, axis=1)
            new = (c != u) & np.all(b != c[:, None, :], axis=1) & (e < np.max(d, axis=1))
            hit = new[:, None, :] & (slot == s[:, None, :])
            b = np.where(hit, c[:, None, :], b); d = np.where(hit, e[:, None, :], d)
    bo = np.ascontiguousarray(b.reshape(8, K, N, V).transpose(2, 0, 1, 3)).reshape(N, 8, K * V)
    do = np.ascontiguousarray(d.reshape(8, K, N, V).transpose(2, 0, 1, 3)).reshape(N, 8, K * V)
    return {"ynb": np.stack([gtable(a) for a in bo]).astype(np.float32), "yd": np.stack([gtable(a) for a in do]).astype(np.float32)}

from concourse.bass import DstId, RemoteDMATransfer
from concourse.mybir import AluOpType as A, ActivationFunctionType as F

NR = 8
SCRATCH = {
    "six": ("dram", [8, 128, 128], "bfloat16"), "sin": ("dram", [8, 128, 32], "int32"),
    "lx": ("dram", [8, 128, 128], "bfloat16"), "ln": ("dram", [8, 128, 32], "int32"),
    "son": ("dram", [8, 128, 32], "float32"), "lon": ("dram", [8, 128, 32], "float32"),
    "sod": ("dram", [8, 128, 32], "float32"), "lod": ("dram", [8, 128, 32], "float32"),
    "Wx": ("sbuf", [128, 8192], "bfloat16"), "W": ("sbuf", [128, 4096], "bfloat16"), "GA": ("sbuf", [128, 4096], "bfloat16"),
    "Xl": ("sbuf", [128, 1024], "bfloat16"), "df": ("sbuf", [128, 8192], "bfloat16"),
    "Z2": ("sbuf", [128, 1024], "bfloat16"), "Z3": ("sbuf", [128, 512], "bfloat16"), "Zb": ("sbuf", [128, 144], "bfloat16"),
    "zt": ("sbuf", [128, 8], "bfloat16"), "bigI": ("sbuf", [128, 128], "bfloat16"), "negI": ("sbuf", [128, 128], "bfloat16"),
    "topI": ("sbuf", [128, 128], "bfloat16"), "J": ("sbuf", [128, 128], "bfloat16"), "Dj": ("sbuf", [128, 128], "bfloat16"),
    "Sj": ("sbuf", [128, 128], "bfloat16"), "selA": ("sbuf", [128, 64], "bfloat16"),
    "tags": ("sbuf", [128, 1024], "bfloat16"), "own": ("sbuf", [128, 256], "float32"),
    "ci": ("sbuf", [128, 2], "int32"), "cf": ("sbuf", [128, 1], "float32"),
    "n32": ("sbuf", [128, 256], "int32"), "Vn": ("sbuf", [128, 256], "int32"), "ns": ("sbuf", [128, 256], "float32"),
    "SS": ("sbuf", [128, 512], "bfloat16"), "am": ("sbuf", [128, 256], "bfloat16"), "T2": ("sbuf", [128, 8, 4, 16], "bfloat16"),
    "offA": ("sbuf", [128, 256], "uint16"), "offB": ("sbuf", [128, 256], "uint16"), "off0": ("sbuf", [128, 256], "uint16"),
    "tq": ("sbuf", [128, 256], "float32"), "cS": ("sbuf", [128, 256], "float32"), "mk": ("sbuf", [128, 1408], "bfloat16"),
    "L": ("sbuf", [128, 256], "int32"), "sb": ("sbuf", [128, 256], "int32"), "uS": ("sbuf", [128, 64], "float32"),
    "ZS": ("sbuf", [128, 256], "float32"), "zs": ("sbuf", [128, 512], "int32"), "ob": ("sbuf", [128, 512], "float32"),
    "R0": ("psum", [128, 512], "float32"), "R1": ("psum", [128, 512], "float32"),
    "R2": ("psum", [128, 512], "float32"), "R3": ("psum", [128, 512], "float32"),
    "E0": ("psum", [128, 512], "float32"), "E1": ("psum", [128, 512], "float32"),
    "P0": ("psum", [128, 512], "float32"), "P1": ("psum", [128, 512], "float32"),
}
SEMAPHORES = ["v", "s", "t", "g", "dn", "dx", "dno", "dxo", "dw", "dv", "ldn", "ldx", "an", "ax", "aon", "aod", "sent",
              "on", "od", "oon", "ood", "fn", "fd"]
PSUM = ("R0", "R1", "R2", "R3", "E0", "E1", "P0", "P1")
S18 = 2.0 ** -18
AV = 64


def rank_program(g, core, T, topo):
    me = T.rank_of(core)
    if me is None:
        return
    Q = {"v": g.vector, "s": g.scalar, "t": g.tensor, "g": g, "y": g.sync}
    cnt = {"v": 0, "s": 0, "t": 0, "g": 0}
    waited = {}
    recs = {}

    def ap(n, lo=0, hi=None, step=1, rows=None):
        hi = SCRATCH[n][1][1] if hi is None else hi
        p = slice(0, 128) if rows is None else slice(rows[0], rows[1])
        return (T[n][p, lo:hi] if step == 1 else T[n][p, lo:hi:step], n, lo, hi)

    def wait(q, sem, val):
        if waited.get((q, sem), 0) < val:
            Q[q].wait_ge(T.sem[sem], val)
            waited[(q, sem)] = val

    def order(q, reads, writes, sem, val):
        need = {}
        for acc, wr in [(r, False) for r in reads] + [(w, True) for w in writes]:
            n, lo, hi = acc[1:4]
            for (rq, rs, rv, rlo, rhi, rw) in recs.get(n, []):
                meet = rlo < hi and lo < rhi and (rw or wr)
                if rq == q and rs == q:
                    dep = meet and q != "t"
                else:
                    dep = meet or n in PSUM
                if dep:
                    need[rs] = max(need.get(rs, 0), rv)
        for s_, v_ in need.items():
            wait(q, s_, v_)
        for acc, wr in [(r, False) for r in reads] + [(w, True) for w in writes]:
            recs.setdefault(acc[1], []).append((q, sem, val, acc[2], acc[3], wr))

    def run(q, reads, writes, call, inc=True):
        order(q, reads, writes, q, cnt[q] + 1)
        ins = call()
        if inc:
            ins.then_inc(T.sem[q], 1)
            cnt[q] += 1

    def gat(win, off):
        return (win[0].indirect(off[0]), win[1], win[2], win[3], off)

    def rd(*xs):
        out = []
        for x in xs:
            out.append(x)
            if len(x) == 5:
                out.append(x[4])
        return out

    def cp(o, i):
        run("v", rd(i), [o], lambda: g.vector.tensor_copy(o[0], i[0]))

    def tt(o, a, b, f):
        run("v", rd(a, b), [o], lambda: g.vector.tensor_tensor(o[0], a[0], b[0], f))

    def ts(o, a, s1, op0, s2=None, op1=None):
        if op1 is None:
            run("v", rd(a), [o], lambda: g.vector.tensor_scalar(o[0], a[0], s1, None, op0))
        else:
            run("v", rd(a), [o], lambda: g.vector.tensor_scalar(o[0], a[0], s1, s2, op0, op1))

    def ms(o, c):
        run("v", [], [o], lambda: g.vector.memset(o[0], c))

    def act(o, i, f, bias=None, scale=None):
        if bias is None:
            run("s", rd(i), [o], lambda: g.scalar.activation(o[0], i[0], f))
        else:
            run("s", rd(i), [o], lambda: g.scalar.activation(o[0], i[0], f, bias=bias, scale=scale))

    def mm(o, l, r, start, stop, inc):
        run("t", [l, r], [o], lambda: g.tensor.matmul(o[0], l[0], r[0], start, stop), inc)

    def dma(q, o, i, sem, val, reads=(), writes=()):
        order(q, list(reads), list(writes), sem, val)
        Q[q].dma_start(o, i).then_inc(T.sem[sem], 16)

    def exchange(src, dst, sem):
        tr = []
        used = []
        for k in range(1, NR):
            r = (me + k) % NR
            d = T.cores[r]
            e = [x for x in topo.engines(core, d) if x not in used][0]
            used.append(e)
            rid, pid = topo.addr(d, core)
            tr.append(RemoteDMATransfer(dst_ids=[DstId(rid=rid, pnc=pid)], dma_engine_mask=1 << e, remote_sem=T.sem[sem],
                                        src=T[src][r], dst=T[dst][me]))
        g.remote_dma_fused(tr, local_sem=T.sem.sent)

    rows = slice(16 * me, 16 * me + 16)
    I = ap("Z2", 0, 128)
    near = range(4 * (me // 4), 4 * (me // 4) + 4)
    far = [r for r in range(NR) if r not in near]

    dma("y", T.sin[:], T.nb[:], "dn", 16)
    dma("s", T.six[:], T.x[:], "dx", 16)
    dma("y", T.ln[me], T.nb[rows, :], "dno", 16)
    dma("s", T.lx[me], T.x[rows, :], "dxo", 16)
    dma("y", T.Wx[0:16, 1024 * me:1024 * me + 1024], T.x[rows, :], "dw", 64)

    ms(I, 1.0)
    ms(ap("zt"), 64.0)
    ms(ap("Z3"), 1.0)
    run("g", [I], [I], lambda: g.affine_select(I[0], I[0], [[-1, 128]], A.is_equal, 0.0, 0, 1))
    zt = ap("zt")
    run("g", [zt], [zt], lambda: g.affine_select(zt[0], zt[0], [[-16, 8]], A.is_ge, 0.0, 0, 1))
    run("g", [], [ap("ci", 0, 1)], lambda: g.iota(T.ci[:, 0:1], [[1, 1]], 0, 1))
    run("g", [zt], [zt], lambda: g.affine_select(zt[0], zt[0], [[16, 8]], A.is_ge, 0.0, 15, -1))
    wait("g", "dn", 16)
    exchange("sin", "ln", "an")
    wait("g", "dx", 16)
    exchange("six", "lx", "ax")
    run("g", [], [ap("own")], lambda: g.iota(T.own[:, :], [[0, 4], [16, 64]], 0, 1, allow_small_or_imprecise_dtypes=True))
    z3 = ap("Z3")
    run("g", [z3], [z3], lambda: g.affine_select(z3[0], z3[0], [[-16, 4], [0, 8], [-1, 16]], A.is_equal, 0.0, -16 * far[0], 1))

    wait("y", "dno", 16)
    wait("y", "an", NR - 1)
    dma("y", T.n32[:, :], T.ln[:], "ldn", 16, writes=[ap("n32")])
    wait("y", "dxo", 16)
    wait("y", "ax", NR - 1)
    for r in near:
        if r != me:
            dma("y", T.Wx[0:16, 1024 * r:1024 * r + 1024], T.lx[r], "dw", 64)
    dma("y", T.Xl[:, :], T.lx[:], "ldx", 16, writes=[ap("Xl")])
    wait("y", "dw", 64)
    half = ap("Wx", 1024 * near[0], 1024 * near[0] + 4096)
    for k in range(1, 8):
        dma("y", T.Wx[16 * k:16 * k + 16, half[2]:half[3]], T.Wx[0:16, half[2]:half[3]], "dv", 112,
            writes=[half] if k == 1 else [])

    ms(ap("Zb"), 0.0)
    for k in range(16):
        ms(ap("tags", 64 * k, 64 * k + 64), float(k + 1 if k < 12 else 16 * (15 - k)))
    cp(ap("Z2", 128, 256), I)
    tt(ap("J", 0, 124), ap("Z2", 0, 124), ap("Z2", 4, 128), A.add)
    ts(ap("bigI"), I, 2.0 ** 20, A.mult)
    ts(ap("negI"), I, -1.0, A.mult)
    ts(ap("topI"), I, -2048.0, A.mult)
    cp(ap("Z2", 256, 512), ap("Z2", 0, 256))
    tt(ap("Dj", 0, 116), ap("J", 8, 124), ap("J", 0, 116), A.subtract)
    tt(ap("Sj", 0, 116), ap("J", 8, 124), ap("J", 0, 116), A.add)
    cp(ap("Zb", 15, 143, 16), zt)
    cp(ap("Z2", 512, 1024), ap("Z2", 0, 512))
    for w in range(4):
        for h in range(2):
            s = 64 * h + (w + h) % 4
            for k, src in enumerate(("Sj", "Dj")):
                c = 16 * w + 8 * k + 4 * h
                ts(ap("selA", c, c + 4), ap(src, s, s + 49, 16), S18 / 2, A.mult)
    ts(ap("ci", 1, 2), ap("ci", 0, 1), 4, A.arith_shift_right)
    ts(ap("cf"), ap("ci", 1, 2), 1008.0, A.mult)
    run("v", [ap("own"), ap("cf")], [ap("own")],
        lambda: g.vector.tensor_scalar(T.own[:, :], T.own[:, :], T.cf[:, 0:1], S18, A.add, A.mult))

    def table():
        cp(ap("SS", 0, 256), ap("n32"))
        tt(ap("SS", 256, 512), ap("n32"), ap("SS", 0, 256), A.subtract)
        ts(ap("ns"), ap("n32"), S18, A.mult)
        for j in range(8):
            for a in range(2):
                mm(ap(("R3", "E0")[j // 4], 64 * (j % 4), 64 * (j % 4) + 64, rows=(64 * a, 64 * a + 64)), ap("SS", j, 512, 8),
                   ap("Z2", 64 * a, 64 * a + 64), True, True, j % 4 == 3 and a == 1)
        act(ap("am"), ap("ns"), F.Sign, bias=-4095.5, scale=2.0 ** 18)
        cp((T.T2[:, 0:4, :, :], "T2", 0, 1), ap("R3", 0, 256))
        act((T.T2[:, 4:8, :, :], "T2", 1, 2), ap("E0", 0, 256), F.Copy)
        for h in range(2):
            o = ap("E1", 128 * h, 128 * h + 128)
            mm(o, ap("SS", 128 * h, 128 * h + 128), I, True, False, False)
            mm(o, ap("SS", 256 + 128 * h, 384 + 128 * h), I, False, False, False)
            mm(o, ap("am", 128 * h, 128 * h + 128), ap("topI"), False, True, h == 1)
        ts(ap("offA"), ap("E1", 0, 256), -2048.0, A.add)
        for b in range(8):
            bank = "R%d" % (b % 4)
            for k in range(4):
                mm(ap(bank, 128 * k, 128 * k + 128), ap("Z2", 4 * (b % 2) + k, 1024, 8), (T.T2[:, :, b // 2, :], "T2", 0, 2),
                   True, True, k == 3)
            if b % 2 == 0:
                cp(ap("W", 512 * b, 512 * b + 512), ap(bank))
            else:
                act(ap("W", 512 * b, 512 * b + 512), ap(bank), F.Copy)

    def gatherA(q, c0, c1):
        o, i = ap("GA", 16 * c0, 16 * c1), gat(ap("W"), ap("offA", c0, c1))
        if q == "v":
            cp(o, i)
        else:
            act(o, i, F.Copy)

    def convA(t, h):
        w = (2 * h + t) % 4
        for p in range(16):
            mm(ap("E%d" % h, p, 256, 16), ap("GA", 2048 * h + p, 2048 * h + 2048, 16), ap("selA", 16 * w, 16 * w + 16),
               True, True, p == 15)

    def nop():
        return None

    def choose(h, fill=(nop, nop, nop)):
        c = (128 * h, 128 * h + 128)
        tt(ap("tq", *c), ap("E%d" % h, 128, 256), ap("am", *c), A.mult)
        fill[0]()
        tt(ap("P0", *c), ap("E%d" % h, 0, 128), ap("tq", *c), A.add)
        fill[1]()
        ts(ap("offB", *c), ap("P0", *c), 2.0 ** 18, A.mult)
        fill[2]()

    def dfb(k, h0=0, h1=2):
        return ap("df", 1024 * k + 512 * h0, 1024 * k + 512 * h1)

    def offs(off, i, h0, h1):
        return ap(off, 64 * i + 32 * h0, 64 * i + 32 * h1)

    def diffV(k, off, i, h0=0, h1=2):
        tt(dfb(k, h0, h1), gat(ap("Wx"), offs(off, i, h0, h1)), ap("Xl", 512 * h0, 512 * h1), A.subtract)

    def absS(k, h0=0, h1=2):
        act(dfb(k, h0, h1), dfb(k, h0, h1), F.Abs)

    def gatherS(k, off, i, h0=0, h1=2):
        act(dfb(k, h0, h1), gat(ap("Wx"), offs(off, i, h0, h1)), F.Copy)

    def subT(k, b0, h0=0, h1=2):
        for h in range(h0, h1):
            o = ap("R%d" % (b0 + h))
            mm(o, ap("negI"), ap("Xl", 512 * h, 512 * h + 512), True, False, False)
            mm(o, I, dfb(k, h, h + 1), False, True, True)

    def absP(k, b0, h0=0, h1=2):
        for h in range(h0, h1):
            act(dfb(k, h, h + 1), ap("R%d" % (b0 + h)), F.Abs)

    def masks():
        cp(ap("cS", 0, 192), ap("P0", 0, 192))
        tt(ap("mk", 0, 256), ap("P0", 0, 256), ap("own"), A.is_equal)
        for k in range(1, 4):
            n = 256 - 64 * k
            tt(ap("mk", 256 * k, 256 * k + n), ap("P0", 0, n), ap("ns", 64 * k, 256), A.is_equal)
            tt(ap("mk", 256 * k + n, 256 * k + 256), ap("P0", n, 256), ap("ns", 0, 64 * k), A.is_equal)
        tt(ap("mk", 1024, 1216), ap("P0", 64, 256), ap("cS", 0, 192), A.is_equal)
        tt(ap("mk", 1216, 1344), ap("P0", 128, 256), ap("cS", 0, 128), A.is_equal)
        tt(ap("mk", 1344, 1408), ap("P0", 192, 256), ap("cS", 0, 64), A.is_equal)

    def convB(k, o, tag, i=None, late_masks=False):
        sums = [(ap("Zb", 15 - p, 143 - p), ap("df", 1024 * k + p, 1024 * k + 1024, 16)) for p in range(16)]
        at = [] if i is None else ([256 * m + 64 * i for m in range(4)]
                                   + [(1024, 1216, 1344)[m - 1] + 64 * (i - m) for m in range(1, i + 1)])
        hits = [(ap("bigI"), ap("mk", c, c + 64)) for c in at]
        terms = [(I, ap("tags", 64 * tag, 64 * tag + 64))] + (sums + hits if late_masks else hits + sums)
        for n, (l, r) in enumerate(terms):
            mm(o, l, r, n == 0, n == len(terms) - 1, n == len(terms) - 1)

    def Lk(k):
        return ap("L", 64 * k, 64 * k + 64)

    def Pk(k):
        return ap("P1", 64 * k, 64 * k + 64)

    def select(t, i, E, fill=()):
        fill = list(fill) + [nop] * 5
        sb = ap("sb", 0, 64)
        z = ap("ZS", 64 * i, 64 * i + 64)
        fill[0]()
        ts(sb, Lk(0), 48, A.bitwise_and)
        fill[1]()
        tt(Pk(0), Lk(0), E, A.subtract)
        fill[2]()
        tt(ap("uS"), Pk(0), sb, A.min)
        fill[3]()
        if i < 3:
            tt(Pk(1), ap("uS"), E, A.add)
        tt(z, ap("uS"), ap("P0", 64 * i, 64 * i + 64), A.add)
        if i == 3:
            tt(Lk(0), ap("uS"), E, A.add)
        for s in range(4):
            act(ap("R%d" % (i % 2), 64 * s, 64 * s + 64), z, F.Abs,
                bias=float((14 - 4 * t - i) * 8192 - 16 * (3 - s) * 2 ** 18), scale=2.0 ** 18)
        fill[4]()

    def op(o, a, b, f):
        return lambda: tt(o, a, b, f)

    def follow(i):
        tt(ap("Vn"), ap("R%d" % (i % 2), 0, 256), ap("Vn"), A.min)

    def sort4(z, out):
        h0, l0, m2 = ap("zs", 256, 320), ap("zs", 320, 384), ap("zs", 384, 448)
        return [op(h0, z(0), z(2), A.max), op(Pk(4), z(1), z(3), A.max), op(l0, z(0), z(2), A.min), op(Pk(5), z(1), z(3), A.min),
                op(Pk(6), h0, Pk(4), A.min), op(out(0), h0, Pk(4), A.max), op(m2, l0, Pk(5), A.max),
                op(out(3), l0, Pk(5), A.min), op(out(1), m2, Pk(6), A.max), op(out(2), m2, Pk(6), A.min)]

    def every(calls):
        for c in calls:
            c()

    def selects(t, bank, s2, s3):
        E = [ap("E%d" % bank(i), 0, 64) for i in range(4)]
        x2, x3 = (Pk(3), Pk(7)) if t < 2 else (Lk(2), Lk(3))
        s2()
        select(t, 0, E[0])
        tt(Lk(0), Pk(1), Lk(1), A.max)
        tt(Pk(2), Pk(1), Lk(1), A.min)
        convB(2, E[2], 4 * t + 2, 2)
        s3()
        select(t, 1, E[1], [nop, op(Pk(3), Pk(2), Lk(2), A.min), op(Lk(1), Pk(2), Lk(2), A.max),
                            lambda: every([op(Lk(2), Pk(3), Lk(3), A.max), op(x3, Pk(3), Lk(3), A.min)]), lambda: follow(0)])
        tt(Lk(0), Pk(1), Lk(1), A.max)
        tt(Pk(2), Pk(1), Lk(1), A.min)
        convB(3, E[3], 4 * t + 3, 3)
        select(t, 2, E[2], [nop, nop, op(Lk(1), Pk(2), Lk(2), A.max), op(x2, Pk(2), Lk(2), A.min), lambda: follow(1)])
        tt(Lk(0), Pk(1), Lk(1), A.max)
        select(t, 3, E[3], [nop, nop, op(Lk(1), Pk(1), Lk(1), A.min), lambda: follow(2)])

    table()
    gatherA("s", 0, 128)
    gatherA("s", 128, 256)
    cp(ap("off0"), ap("n32"))
    ts(ap("Vn"), ap("n32"), float(15 * 8192), A.add)
    for n in range(8):
        bank = ap("R%d" % (n % 4))
        mm(bank, ap("Z3", 128 * (n // 2), 128 * (n // 2) + 128), ap("Xl", 512 * (n % 2), 512 * (n % 2) + 512), True, True, True)
        cp(ap("Wx", 1024 * far[0] + 512 * n, 1024 * far[0] + 512 * n + 512), bank)
    convA(0, 0)
    diffV(4, "off0", 0)
    convA(0, 1)
    diffV(5, "off0", 1)
    gatherS(6, "off0", 2)
    choose(0)
    choose(1)
    subT(6, 0)
    absS(4)
    convB(4, ap("E0", 0, 64), 12)
    diffV(0, "offB", 0)
    absS(5)
    convB(5, ap("E0", 64, 128), 13)
    gatherS(7, "off0", 3)
    subT(7, 2)
    absP(6, 0)
    convB(6, ap("E0", 128, 192), 14)
    diffV(1, "offB", 1)
    absP(7, 2)
    convB(7, ap("E0", 192, 256), 15)
    masks()
    absS(0)
    convB(0, ap("E1", 0, 64), 0, 0)
    diffV(2, "offB", 2)
    absS(1)
    gatherS(3, "offB", 3)
    cp(ap("zs", 0, 128), ap("E0", 0, 128))
    every(sort4(lambda k: ap("zs", 64 * k, 64 * k + 64) if k < 2 else ap("E0", 64 * k, 64 * k + 64), Lk))
    convB(1, ap("E0", 0, 64), 1, 1)
    subT(3, 2)
    selects(0, lambda i: (i + 1) % 2, lambda: absS(2), lambda: absP(3, 2))

    for t in (1, 2):
        follow(3)
        ts(ap("n32"), ap("Vn"), 8191, A.bitwise_and)
        table()
        gatherA("v", 0, AV)
        gatherA("s", AV, 128)
        convA(t, 0)
        gatherA("s", 128, 256)
        srt = sort4(lambda k: (Lk(0), Lk(1), Pk(3), Pk(7))[k], Lk)
        every(srt[:7])
        choose(0, srt[7:])
        convA(t, 1)
        diffV(0, "offB", 0)
        diffV(1, "offB", 1)
        choose(1)
        absS(0)
        absS(1)
        masks()
        diffV(2, "offB", 2, 0, 1)
        convB(0, ap("E0", 0, 64), 4 * t, 0, True)
        gatherS(2, "offB", 2, 1, 2)
        convB(1, ap("E1", 0, 64), 4 * t + 1, 1, True)
        subT(2, 0, 1, 2)
        gatherS(3, "offB", 3)
        subT(3, 2)
        selects(t, lambda i: i % 2, lambda: (absS(2, 0, 1), absP(2, 0, 1, 2)), lambda: absP(3, 2))

    ts(ap("sb"), ap("L"), 48, A.bitwise_and)
    ts(ap("P1", 0, 256), ap("sb"), 2.0 ** 14, A.mult)
    follow(3)
    tt(ap("zs", 0, 128), ap("P1", 0, 128), ap("L", 0, 128), A.add)
    ts(ap("n32"), ap("Vn"), 8191, A.bitwise_and)
    tt(ap("P1", 128, 256), ap("P1", 128, 256), ap("L", 128, 256), A.add)
    cp(ap("ob", 0, 256), ap("n32"))
    dma("y", T.son[:], T.ob[:, 0:256], "on", 16, reads=[ap("ob", 0, 256)])
    dma("y", T.lon[me], T.ob[rows, 0:256], "oon", 16)
    every(sort4(lambda k: ap("zs", 64 * k, 64 * k + 64) if k < 2 else Pk(k), Lk))
    ts(ap("sb"), ap("L"), 6, A.arith_shift_right, 4095, A.bitwise_and)
    cp(ap("ob", 256, 512), ap("sb"))
    dma("s", T.sod[:], T.ob[:, 256:512], "od", 16, reads=[ap("ob", 256, 512)])
    dma("s", T.lod[me], T.ob[rows, 256:512], "ood", 16)
    wait("g", "on", 16)
    exchange("son", "lon", "aon")
    wait("g", "od", 16)
    exchange("sod", "lod", "aod")
    wait("y", "oon", 16)
    wait("y", "aon", NR - 1)
    dma("y", T.ynb[:, :], T.lon[:], "fn", 16)
    wait("s", "ood", 16)
    wait("s", "aod", NR - 1)
    dma("s", T.yd[:, :], T.lod[:], "fd", 16)
    wait("y", "fn", 16)
    wait("s", "fd", 16)
    wait("g", "sent", 4 * (NR - 1))
    for q in ("v", "s", "t", "g"):
        wait("g", q, cnt[q])
